import numpy as np
import ml_dtypes


def mxq(x, axis, fmt="e4m3"):
    dtype, down = {"e4m3": (ml_dtypes.float8_e4m3fn, 7), "e5m2": (ml_dtypes.float8_e5m2, 14)}[fmt]
    v = np.moveaxis(np.asarray(x, np.float32).astype(ml_dtypes.bfloat16).astype(np.float64), axis, -1)
    blocks = v.reshape(v.shape[:-1] + (-1, 32))
    amax = np.abs(blocks).max(-1, keepdims=True)
    byte = np.maximum(np.where(amax > 0, np.frexp(amax)[1] - 1 + 127, 0) - down, 1)
    scale = np.exp2(byte - 127.0)
    codes = (blocks / scale).astype(np.float32).astype(dtype).astype(np.float64)
    return np.moveaxis((codes * scale).reshape(v.shape), -1, axis)


WIDE = False


def mx_kscale(k):
    if not WIDE:
        return np.ones(k)
    levels = np.array([10, -10, 5, -5, 0])
    if k % 512:
        return np.exp2(np.random.permutation(np.resize(levels, k // 32))).repeat(32)
    a = np.empty((k // 512, 16))
    for p in range(k // 512):
        a[p, :8] = np.random.permutation(np.resize(levels, 8))
        for g in range(8):
            far = levels[np.abs(levels - a[p, g]) >= 10]
            a[p, g + 8] = far[np.random.randint(len(far))]
    return np.exp2(a.ravel()).repeat(32)


def f64(x):
    return np.asarray(x).astype(np.float64)


def striped(idx):
    return np.tile(idx.reshape(-1, 16).T, (8, 1)).astype(np.uint16)


def unstriped(offs):
    return offs[:16].T.reshape(-1).astype(np.int64)


def gelu(v):
    return 0.5 * v * (1.0 + np.tanh(np.sqrt(2.0 / np.pi) * (v + 0.044715 * v**3)))


K, T, D, S, V, H, N = 512, 2048, 2, 512, 256, 512, 512


def setup_inputs():
    n = np.random.standard_normal
    s = mx_kscale(K)[:, None]
    u = mx_kscale(H)
    return {
        "xT": (n((K, T)) * s).astype(np.float32),
        "w1": (n((K, H)) / np.sqrt(K) / s * u).astype(np.float32),
        "w2": (n((H, N)) / np.sqrt(H) / u[:, None]).astype(np.float32),
        "gate": np.tile(np.random.uniform(0.2, 1.0, (D, 1, V)) / np.sqrt(D), (1, N, 1)).astype(np.float32),
        "offs": striped(np.random.permutation(T)[:S]),
        "pos1": striped(np.random.permutation(S)[:V]),
        "pos2": striped(np.random.permutation(S)[:V]),
    }


def reference(xT, w1, w2, gate, offs, pos1, pos2):
    idx = unstriped(offs)
    xq = mxq(f64(xT)[:, idx], 0, "e4m3")
    h = gelu(mxq(f64(w1), 0, "e4m3").T @ xq)
    y = mxq(f64(w2), 0, "e4m3").T @ mxq(h, 0, "e4m3")
    return sum(f64(gate[d]) * y[:, unstriped(p)] for d, p in enumerate((pos1, pos2)))

@@ -1,0 +1,194 @@
+from contextlib import ExitStack
+
+import concourse.mybir as mybir
+
+K, T, D, S, V, H, N = 512, 2048, 2, 512, 256, 512, 512
+FLOPS = 2 * S * (K * H + H * N) + 3 * N * V
+
+F32 = mybir.dt.float32
+BF16 = mybir.dt.bfloat16
+U32 = mybir.dt.uint32
+U16 = mybir.dt.uint16
+U8 = mybir.dt.uint8
+FP8X4 = mybir.dt.float8_e4m3fn_x4
+ACT = mybir.ActivationFunctionType
+ALU = mybir.AluOpType
+
+P = 128
+PACK = 4
+BLOCKS = N // P
+
+
+def tile_picked_sub_mlp_gelu_sub_e_kernel(tc, xT, w1, w2, gate, offs, pos1, pos2, out):
+    nc = tc.nc
+    with ExitStack() as ctx:
+        lists = ctx.enter_context(tc.tile_pool(name="lists", bufs=1))
+        keep = ctx.enter_context(tc.tile_pool(name="keep", bufs=1))
+        psum = ctx.enter_context(tc.psum_pool(name="psum", bufs=1))
+
+        offs_sb = lists.tile([P, S // 16], U16, name="offs_sb")
+        pos_sb = [lists.tile([P, V // 16], U16, name=f"pos_sb{d}") for d in range(D)]
+
+        warm = keep.tile([P, 1], F32, name="warm")
+        nc.vector.memset(warm[:], 0.0)
+        warm_out = keep.tile([P, 1], F32, name="warm_out")
+        nc.scalar.activation(warm_out[:], warm[:], ACT.Gelu_apprx_tanh)
+
+        x_rows = xT.rearrange("(p j) t -> p j t", j=PACK)
+        w1_rows = w1.rearrange("(p j) c -> p j c", j=PACK)
+        w2_rows = w2.rearrange("(p j) c -> p j c", j=PACK)
+        x_raw = [keep.tile([P, T], F32, name=f"x_raw{j}") for j in range(PACK)]
+        w1_raw = keep.tile([P, PACK, H], F32, name="w1_raw")
+        w2_raw = [keep.tile([P, PACK, N // 2], F32, name=f"w2_raw{u}") for u in range(2)]
+        gate_sb = [keep.tile([P, D, V], F32, name=f"gate_sb{b}") for b in range(BLOCKS)]
+        nc.sync.dma_start(x_raw[0][:], x_rows[:, 0, :])
+        nc.sync.dma_start(offs_sb[:], offs)
+        nc.sync.dma_start(x_raw[1][:], x_rows[:, 1, :])
+        nc.sync.dma_start(w1_raw[:], w1_rows)
+        for j in range(2, PACK):
+            nc.sync.dma_start(x_raw[j][:], x_rows[:, j, :])
+        for u in range(2):
+            nc.sync.dma_start(w2_raw[u][:], w2_rows[:, :, u * N // 2 : (u + 1) * N // 2])
+        nc.sync.dma_start(pos_sb[0][:], pos1)
+        nc.sync.dma_start(pos_sb[1][:], pos2)
+        for b in range(BLOCKS):
+            nc.sync.dma_start(gate_sb[b][:], gate[:, b * P : (b + 1) * P, :].rearrange("d p v -> p d v"))
+
+        half = S // 2
+        x_grp = [keep.tile([P, half, PACK], BF16, name=f"x_grp{i}", align_bytes=64) for i in range(2)]
+        x_codes = keep.tile([P, S], U32, name="x_codes", align_bytes=64)
+        x_scales = keep.tile([P, S], U8, name="x_scales", align_bytes=64)
+
+        def gather(j, i):
+            nc.vector.tensor_copy(
+                x_grp[i][:, :, j], x_raw[j][:].indirect(offs_sb[:, i * half // 16 : (i + 1) * half // 16])
+            )
+
+        def x_quant(q):
+            toks = slice(q * P, (q + 1) * P)
+            r0 = q % 2 * P
+            nc.vector.quantize_mx(
+                out=x_codes[:, toks].bitcast(FP8X4),
+                scales=x_scales[:, toks],
+                in_=x_grp[q // 2][:, r0 : r0 + P, :].rearrange("p s j -> p (s j)"),
+            )
+
+        for j in range(PACK - 1):
+            for i in range(2):
+                gather(j, i)
+
+        w1_grp = keep.tile([P, PACK, P, PACK], BF16, name="w1_grp", align_bytes=64)
+        for m0 in range(0, P, P // 2):
+            nc.scalar.copy(
+                w1_grp[:, :, m0 : m0 + P // 2, :].rearrange("p t m j -> p m t j"),
+                w1_raw[:, :, PACK * m0 : PACK * (m0 + P // 2)].rearrange("p j (m t) -> p m t j", t=PACK),
+            )
+        w1_codes = keep.tile([P, H], U32, name="w1_codes", align_bytes=64)
+        w1_scales = keep.tile([P, H], U8, name="w1_scales", align_bytes=64)
+        nc.vector.quantize_mx(
+            out=w1_codes[:].bitcast(FP8X4), scales=w1_scales[:], in_=w1_grp[:].rearrange("p t m j -> p (t m j)")
+        )
+
+        for i in range(2):
+            gather(PACK - 1, i)
+            x_quant(2 * i)
+            x_quant(2 * i + 1)
+
+        w2_grp = keep.tile([P, N, PACK], BF16, name="w2_grp", align_bytes=64)
+        w2_codes = keep.tile([P, N], U32, name="w2_codes", align_bytes=64)
+        w2_scales = keep.tile([P, N], U8, name="w2_scales", align_bytes=64)
+
+        def w2_part(copy, b):
+            c0 = b * P
+            r0 = c0 % (N // 2)
+            copy(
+                w2_grp[:, c0 : c0 + P, :],
+                w2_raw[b // 2][:, :, r0 : r0 + P].rearrange("p j c -> p c j"),
+            )
+
+        def w2_quant(c0, c1):
+            nc.vector.quantize_mx(
+                out=w2_codes[:, c0:c1].bitcast(FP8X4),
+                scales=w2_scales[:, c0:c1],
+                in_=w2_grp[:, c0:c1, :].rearrange("p c j -> p (c j)"),
+            )
+
+        h_codes = keep.tile([P, S], U32, name="h_codes", align_bytes=64)
+        h_scales = keep.tile([P, S], U8, name="h_scales", align_bytes=64)
+
+        def layer1(q):
+            toks = slice(q * P, (q + 1) * P)
+            acc = psum.tile([P, PACK, P], F32, name=f"acc1_{q}")
+            for t in range(PACK):
+                cols = slice(t * P, (t + 1) * P)
+                nc.tensor.matmul_mx(
+                    out=acc[:, t, :],
+                    lhsT=w1_codes[:, cols].bitcast(FP8X4),
+                    lhsT_scale=w1_scales[:, cols],
+                    rhs=x_codes[:, toks].bitcast(FP8X4),
+                    rhs_scale=x_scales[:, toks],
+                    start=True,
+                    stop=True,
+                )
+            h_grp = keep.tile([P, P, PACK], BF16, name=f"h_grp{q}", align_bytes=64)
+            nc.scalar.activation(h_grp[:], acc[:].rearrange("p t n -> p n t"), ACT.Gelu_apprx_tanh)
+            nc.vector.quantize_mx(
+                out=h_codes[:, toks].bitcast(FP8X4),
+                scales=h_scales[:, toks],
+                in_=h_grp[:].rearrange("p n t -> p (n t)"),
+            )
+
+        y_sb = [keep.tile([P, S], F32, name=f"y_sb{b}") for b in range(BLOCKS)]
+
+        def layer2(acc, b, t0, t1):
+            cols = slice(b * P, (b + 1) * P)
+            nc.tensor.matmul_mx(
+                out=acc,
+                lhsT=w2_codes[:, cols].bitcast(FP8X4),
+                lhsT_scale=w2_scales[:, cols],
+                rhs=h_codes[:, t0:t1].bitcast(FP8X4),
+                rhs_scale=h_scales[:, t0:t1],
+                start=True,
+                stop=True,
+            )
+
+        layer1(0)
+        layer1(1)
+        w2_part(nc.vector.tensor_copy, 0)
+        w2_part(nc.vector.tensor_copy, 1)
+        w2_quant(0, N // 2)
+        w2_part(nc.gpsimd.tensor_copy, 2)
+        w2_part(nc.gpsimd.tensor_copy, 3)
+        layer1(2)
+        layer1(3)
+        w2_quant(N // 2, N)
+        a01 = psum.tile([P, 2, half], F32, name="a01")
+        a23 = psum.tile([P, 2, half], F32, name="a23")
+        layer2(a01[:, 0, :], 0, 0, half)
+        layer2(a01[:, 1, :], 1, 0, half)
+        nc.vector.tensor_copy(y_sb[0][:, 0:half], a01[:, 0, :])
+        nc.vector.tensor_copy(y_sb[1][:, 0:half], a01[:, 1, :])
+        b0 = psum.tile([P, half], F32, name="b0")
+        b1 = psum.tile([P, half], F32, name="b1")
+        b23 = psum.tile([P, 2, half], F32, name="b23", tag="acc1_0")
+        layer2(b0[:], 0, half, S)
+        layer2(b1[:], 1, half, S)
+        layer2(a23[:, 0, :], 2, 0, half)
+        layer2(a23[:, 1, :], 3, 0, half)
+        layer2(b23[:, 0, :], 2, half, S)
+        layer2(b23[:, 1, :], 3, half, S)
+        nc.scalar.copy(y_sb[0][:, half:S], b0[:])
+        nc.scalar.copy(y_sb[1][:, half:S], b1[:])
+        for b in (2, 3):
+            nc.scalar.copy(y_sb[b][:, 0:half], a23[:, b - 2, :])
+            nc.scalar.copy(y_sb[b][:, half:S], b23[:, b - 2, :])
+
+        for b in range(BLOCKS):
+            terms = []
+            for d in range(D):
+                term = keep.tile([P, V], F32, name=f"term{b}_{d}")
+                nc.vector.tensor_tensor(term[:], y_sb[b][:].indirect(pos_sb[d][:]), gate_sb[b][:, d, :], ALU.mult)
+                terms.append(term)
+            total = keep.tile([P, V], F32, name=f"total{b}")
+            nc.vector.tensor_tensor(total[:], terms[0][:], terms[1][:], ALU.add)
+            nc.sync.dma_start(out[b * P : (b + 1) * P, :], total[:])

@@ -55,27 +55,23 @@ def tile_picked_sub_mlp_gelu_sub_e_kernel(tc, xT, w1, w2, gate, offs, pos1, pos2
             nc.sync.dma_start(gate_sb[b][:], gate[:, b * P : (b + 1) * P, :].rearrange("d p v -> p d v"))
 
         half = S // 2
-        x_grp = [keep.tile([P, half, PACK], BF16, name=f"x_grp{i}", align_bytes=64) for i in range(2)]
+        x_grp = keep.tile([P, S, PACK], BF16, name="x_grp", align_bytes=64)
         x_codes = keep.tile([P, S], U32, name="x_codes", align_bytes=64)
         x_scales = keep.tile([P, S], U8, name="x_scales", align_bytes=64)
 
-        def gather(j, i):
-            nc.vector.tensor_copy(
-                x_grp[i][:, :, j], x_raw[j][:].indirect(offs_sb[:, i * half // 16 : (i + 1) * half // 16])
-            )
+        def gather(j):
+            nc.vector.tensor_copy(x_grp[:, :, j], x_raw[j][:].indirect(offs_sb[:]))
 
         def x_quant(q):
             toks = slice(q * P, (q + 1) * P)
-            r0 = q % 2 * P
             nc.vector.quantize_mx(
                 out=x_codes[:, toks].bitcast(FP8X4),
                 scales=x_scales[:, toks],
-                in_=x_grp[q // 2][:, r0 : r0 + P, :].rearrange("p s j -> p (s j)"),
+                in_=x_grp[:, toks, :].rearrange("p s j -> p (s j)"),
             )
 
         for j in range(PACK - 1):
-            for i in range(2):
-                gather(j, i)
+            gather(j)
 
         w1_grp = keep.tile([P, PACK, P, PACK], BF16, name="w1_grp", align_bytes=64)
         for m0 in range(0, P, P // 2):
@@ -89,10 +85,9 @@ def tile_picked_sub_mlp_gelu_sub_e_kernel(tc, xT, w1, w2, gate, offs, pos1, pos2
             out=w1_codes[:].bitcast(FP8X4), scales=w1_scales[:], in_=w1_grp[:].rearrange("p t m j -> p (t m j)")
         )
 
-        for i in range(2):
-            gather(PACK - 1, i)
-            x_quant(2 * i)
-            x_quant(2 * i + 1)
+        gather(PACK - 1)
+        for q in range(S // P):
+            x_quant(q)
 
         w2_grp = keep.tile([P, N, PACK], BF16, name="w2_grp", align_bytes=64)
         w2_codes = keep.tile([P, N], U32, name="w2_codes", align_bytes=64)
@@ -152,33 +147,36 @@ def tile_picked_sub_mlp_gelu_sub_e_kernel(tc, xT, w1, w2, gate, offs, pos1, pos2
                 stop=True,
             )
 
+        w2_part(nc.scalar.copy, 0)
         layer1(0)
         layer1(1)
-        w2_part(nc.vector.tensor_copy, 0)
         w2_part(nc.vector.tensor_copy, 1)
         w2_quant(0, N // 2)
-        w2_part(nc.gpsimd.tensor_copy, 2)
-        w2_part(nc.gpsimd.tensor_copy, 3)
+        w2_part(nc.vector.tensor_copy, 2)
+        w2_part(nc.vector.tensor_copy, 3)
+        w2_quant(N // 2, N)
         layer1(2)
         layer1(3)
-        w2_quant(N // 2, N)
         a01 = psum.tile([P, 2, half], F32, name="a01")
         a23 = psum.tile([P, 2, half], F32, name="a23")
+        q2_0 = psum.tile([P, P], F32, name="q2_0", tag="acc1_0")
+        q3_0 = psum.tile([P, P], F32, name="q3_0")
+        b1 = psum.tile([P, half], F32, name="b1")
+        b23 = psum.tile([P, 2, half], F32, name="b23", tag="acc1_1")
         layer2(a01[:, 0, :], 0, 0, half)
         layer2(a01[:, 1, :], 1, 0, half)
         nc.vector.tensor_copy(y_sb[0][:, 0:half], a01[:, 0, :])
-        nc.vector.tensor_copy(y_sb[1][:, 0:half], a01[:, 1, :])
-        b0 = psum.tile([P, half], F32, name="b0")
-        b1 = psum.tile([P, half], F32, name="b1")
-        b23 = psum.tile([P, 2, half], F32, name="b23", tag="acc1_0")
-        layer2(b0[:], 0, half, S)
+        layer2(q2_0[:], 0, half, half + P)
+        nc.vector.tensor_copy(y_sb[0][:, half : half + P], q2_0[:])
+        layer2(q3_0[:], 0, half + P, S)
+        nc.scalar.copy(y_sb[0][:, half + P : S], q3_0[:])
         layer2(b1[:], 1, half, S)
-        layer2(a23[:, 0, :], 2, 0, half)
-        layer2(a23[:, 1, :], 3, 0, half)
-        layer2(b23[:, 0, :], 2, half, S)
-        layer2(b23[:, 1, :], 3, half, S)
-        nc.scalar.copy(y_sb[0][:, half:S], b0[:])
+        nc.scalar.copy(y_sb[1][:, 0:half], a01[:, 1, :])
         nc.scalar.copy(y_sb[1][:, half:S], b1[:])
+        for b in (2, 3):
+            layer2(a23[:, b - 2, :], b, 0, half)
+        for b in (2, 3):
+            layer2(b23[:, b - 2, :], b, half, S)
         for b in (2, 3):
             nc.scalar.copy(y_sb[b][:, 0:half], a23[:, b - 2, :])
             nc.scalar.copy(y_sb[b][:, half:S], b23[:, b - 2, :])

@@ -1,6 +1,7 @@
 from contextlib import ExitStack
 
 import concourse.mybir as mybir
+from concourse.masks import make_identity
 
 K, T, D, S, V, H, N = 512, 2048, 2, 512, 256, 512, 512
 FLOPS = 2 * S * (K * H + H * N) + 3 * N * V
@@ -59,8 +60,8 @@ def tile_picked_sub_mlp_gelu_sub_e_kernel(tc, xT, w1, w2, gate, offs, pos1, pos2
         x_codes = keep.tile([P, S], U32, name="x_codes", align_bytes=64)
         x_scales = keep.tile([P, S], U8, name="x_scales", align_bytes=64)
 
-        def gather(j):
-            nc.vector.tensor_copy(x_grp[:, :, j], x_raw[j][:].indirect(offs_sb[:]))
+        def gather(j, s0, s1):
+            nc.vector.tensor_copy(x_grp[:, s0:s1, j], x_raw[j][:].indirect(offs_sb[:, s0 // 16 : s1 // 16]))
 
         def x_quant(q):
             toks = slice(q * P, (q + 1) * P)
@@ -71,11 +72,11 @@ def tile_picked_sub_mlp_gelu_sub_e_kernel(tc, xT, w1, w2, gate, offs, pos1, pos2
             )
 
         for j in range(PACK - 1):
-            gather(j)
+            gather(j, 0, S)
 
         w1_grp = keep.tile([P, PACK, P, PACK], BF16, name="w1_grp", align_bytes=64)
-        for m0 in range(0, P, P // 2):
-            nc.scalar.copy(
+        for copy, m0 in ((nc.scalar.copy, 0), (nc.vector.tensor_copy, P // 2)):
+            copy(
                 w1_grp[:, :, m0 : m0 + P // 2, :].rearrange("p t m j -> p m t j"),
                 w1_raw[:, :, PACK * m0 : PACK * (m0 + P // 2)].rearrange("p j (m t) -> p m t j", t=PACK),
             )
@@ -85,27 +86,33 @@ def tile_picked_sub_mlp_gelu_sub_e_kernel(tc, xT, w1, w2, gate, offs, pos1, pos2
             out=w1_codes[:].bitcast(FP8X4), scales=w1_scales[:], in_=w1_grp[:].rearrange("p t m j -> p (t m j)")
         )
 
-        gather(PACK - 1)
-        for q in range(S // P):
-            x_quant(q)
+        gather(PACK - 1, 0, half)
+        x_quant(0)
+        x_quant(1)
+        gather(PACK - 1, half - 32, S)
+        x_quant(2)
+        x_quant(3)
 
-        w2_grp = keep.tile([P, N, PACK], BF16, name="w2_grp", align_bytes=64)
+        ident = keep.tile([P, P], BF16, name="ident")
+        make_identity(nc, ident[:])
+        warm_ps = psum.tile([P, P], BF16, name="warm_ps", tag="y_tail1")
+        w1_flat = w1_grp[:].rearrange("p t m j -> p (t m j)")
+        for i in range(20):
+            c0 = i % 16 * P
+            nc.tensor.transpose(warm_ps[:], w1_flat[:, c0 : c0 + P], ident[:])
+
         w2_codes = keep.tile([P, N], U32, name="w2_codes", align_bytes=64)
         w2_scales = keep.tile([P, N], U8, name="w2_scales", align_bytes=64)
 
-        def w2_part(copy, b):
+        def w2_block(copy, b, tag):
             c0 = b * P
             r0 = c0 % (N // 2)
-            copy(
-                w2_grp[:, c0 : c0 + P, :],
-                w2_raw[b // 2][:, :, r0 : r0 + P].rearrange("p j c -> p c j"),
-            )
-
-        def w2_quant(c0, c1):
+            w2_grp = keep.tile([P, P, PACK], BF16, name=f"w2_grp{b}", tag=tag, align_bytes=64)
+            copy(w2_grp[:], w2_raw[b // 2][:, :, r0 : r0 + P].rearrange("p j c -> p c j"))
             nc.vector.quantize_mx(
-                out=w2_codes[:, c0:c1].bitcast(FP8X4),
-                scales=w2_scales[:, c0:c1],
-                in_=w2_grp[:, c0:c1, :].rearrange("p c j -> p (c j)"),
+                out=w2_codes[:, c0 : c0 + P].bitcast(FP8X4),
+                scales=w2_scales[:, c0 : c0 + P],
+                in_=w2_grp[:].rearrange("p c j -> p (c j)"),
             )
 
         h_codes = keep.tile([P, S], U32, name="h_codes", align_bytes=64)
@@ -125,7 +132,7 @@ def tile_picked_sub_mlp_gelu_sub_e_kernel(tc, xT, w1, w2, gate, offs, pos1, pos2
                     start=True,
                     stop=True,
                 )
-            h_grp = keep.tile([P, P, PACK], BF16, name=f"h_grp{q}", align_bytes=64)
+            h_grp = keep.tile([P, P, PACK], BF16, name=f"h_grp{q}", tag=f"h_grp{q}", align_bytes=64)
             nc.scalar.activation(h_grp[:], acc[:].rearrange("p t n -> p n t"), ACT.Gelu_apprx_tanh)
             nc.vector.quantize_mx(
                 out=h_codes[:, toks].bitcast(FP8X4),
@@ -147,46 +154,51 @@ def tile_picked_sub_mlp_gelu_sub_e_kernel(tc, xT, w1, w2, gate, offs, pos1, pos2
                 stop=True,
             )
 
-        w2_part(nc.scalar.copy, 0)
+        head = S - P
+        y_head = [psum.tile([P, head], F32, name=f"y_head{b}") for b in range(2)]
+        y_tail = [psum.tile([P, P], F32, name=f"y_tail{b}", tag=f"y_tail{b}") for b in range(2)]
+        w2_block(nc.scalar.copy, 0, "w2_grp0")
         layer1(0)
         layer1(1)
-        w2_part(nc.vector.tensor_copy, 1)
-        w2_quant(0, N // 2)
-        w2_part(nc.vector.tensor_copy, 2)
-        w2_part(nc.vector.tensor_copy, 3)
-        w2_quant(N // 2, N)
+        w2_block(nc.vector.tensor_copy, 1, "w2_grp1")
+        w2_block(nc.vector.tensor_copy, 2, "w2_grp2")
         layer1(2)
         layer1(3)
-        a01 = psum.tile([P, 2, half], F32, name="a01")
-        a23 = psum.tile([P, 2, half], F32, name="a23")
-        q2_0 = psum.tile([P, P], F32, name="q2_0", tag="acc1_0")
-        q3_0 = psum.tile([P, P], F32, name="q3_0")
-        b1 = psum.tile([P, half], F32, name="b1")
-        b23 = psum.tile([P, 2, half], F32, name="b23", tag="acc1_1")
-        layer2(a01[:, 0, :], 0, 0, half)
-        layer2(a01[:, 1, :], 1, 0, half)
-        nc.vector.tensor_copy(y_sb[0][:, 0:half], a01[:, 0, :])
-        layer2(q2_0[:], 0, half, half + P)
-        nc.vector.tensor_copy(y_sb[0][:, half : half + P], q2_0[:])
-        layer2(q3_0[:], 0, half + P, S)
-        nc.scalar.copy(y_sb[0][:, half + P : S], q3_0[:])
-        layer2(b1[:], 1, half, S)
-        nc.scalar.copy(y_sb[1][:, 0:half], a01[:, 1, :])
-        nc.scalar.copy(y_sb[1][:, half:S], b1[:])
-        for b in (2, 3):
-            layer2(a23[:, b - 2, :], b, 0, half)
-        for b in (2, 3):
-            layer2(b23[:, b - 2, :], b, half, S)
-        for b in (2, 3):
-            nc.scalar.copy(y_sb[b][:, 0:half], a23[:, b - 2, :])
-            nc.scalar.copy(y_sb[b][:, half:S], b23[:, b - 2, :])
+        w2_block(nc.vector.tensor_copy, 3, "w2_grp3")
+        for b in range(2):
+            layer2(y_head[b][:, 0:half], b, 0, half)
+            layer2(y_head[b][:, half:head], b, half, head)
+        nc.vector.tensor_copy(y_sb[0][:, 0:head], y_head[0][:])
+        for b in range(2):
+            layer2(y_tail[b][:], b, head, S)
+        nc.scalar.copy(y_sb[0][:, head:S], y_tail[0][:])
+        nc.scalar.copy(y_sb[1][:, 0:head], y_head[1][:])
+        nc.scalar.copy(y_sb[1][:, head:S], y_tail[1][:])
+        for b in range(2, BLOCKS):
+            y_acc = psum.tile([P, S], F32, name=f"y_acc{b}", tag=f"acc1_{b - 2}")
+            layer2(y_acc[:], b, 0, S)
+            nc.scalar.copy(y_sb[b][:], y_acc[:])
 
-        for b in range(BLOCKS):
-            terms = []
+        terms = [keep.tile([P, BLOCKS, V], F32, name=f"terms{d}") for d in range(D)]
+        total = keep.tile([P, BLOCKS, V], F32, name="total")
+        out_rows = out.rearrange("(b p) v -> p b v", p=P)
+
+        def term(b, d):
+            nc.vector.tensor_tensor(
+                terms[d][:, b, :], y_sb[b][:].indirect(pos_sb[d][:]), gate_sb[b][:, d, :], ALU.mult
+            )
+
+        def finish(b0, b1):
+            nc.vector.tensor_tensor(total[:, b0:b1, :], terms[0][:, b0:b1, :], terms[1][:, b0:b1, :], ALU.add)
+            nc.sync.dma_start(out_rows[:, b0:b1, :], total[:, b0:b1, :])
+
+        for b in (0, 1):
             for d in range(D):
-                term = keep.tile([P, V], F32, name=f"term{b}_{d}")
-                nc.vector.tensor_tensor(term[:], y_sb[b][:].indirect(pos_sb[d][:]), gate_sb[b][:, d, :], ALU.mult)
-                terms.append(term)
-            total = keep.tile([P, V], F32, name=f"total{b}")
-            nc.vector.tensor_tensor(total[:], terms[0][:], terms[1][:], ALU.add)
-            nc.sync.dma_start(out[b * P : (b + 1) * P, :], total[:])
+                term(b, d)
+        term(2, 0)
+        finish(0, 2)
+        term(2, 1)
+        term(3, 0)
+        finish(2, 3)
+        term(3, 1)
+        finish(3, 4)

@@ -42,11 +42,9 @@ def tile_picked_sub_mlp_gelu_sub_e_kernel(tc, xT, w1, w2, gate, offs, pos1, pos2
         w1_raw = keep.tile([P, PACK, H], F32, name="w1_raw")
         w2_raw = [keep.tile([P, PACK, N // 2], F32, name=f"w2_raw{u}") for u in range(2)]
         gate_sb = [keep.tile([P, D, V], F32, name=f"gate_sb{b}") for b in range(BLOCKS)]
-        nc.sync.dma_start(x_raw[0][:], x_rows[:, 0, :])
-        nc.sync.dma_start(offs_sb[:], offs)
-        nc.sync.dma_start(x_raw[1][:], x_rows[:, 1, :])
         nc.sync.dma_start(w1_raw[:], w1_rows)
-        for j in range(2, PACK):
+        nc.sync.dma_start(offs_sb[:], offs)
+        for j in range(PACK):
             nc.sync.dma_start(x_raw[j][:], x_rows[:, j, :])
         for u in range(2):
             nc.sync.dma_start(w2_raw[u][:], w2_rows[:, :, u * N // 2 : (u + 1) * N // 2])
@@ -71,9 +69,6 @@ def tile_picked_sub_mlp_gelu_sub_e_kernel(tc, xT, w1, w2, gate, offs, pos1, pos2
                 in_=x_grp[:, toks, :].rearrange("p s j -> p (s j)"),
             )
 
-        for j in range(PACK - 1):
-            gather(j, 0, S)
-
         w1_grp = keep.tile([P, PACK, P, PACK], BF16, name="w1_grp", align_bytes=64)
         for copy, m0 in ((nc.scalar.copy, 0), (nc.vector.tensor_copy, P // 2)):
             copy(
@@ -86,6 +81,9 @@ def tile_picked_sub_mlp_gelu_sub_e_kernel(tc, xT, w1, w2, gate, offs, pos1, pos2
             out=w1_codes[:].bitcast(FP8X4), scales=w1_scales[:], in_=w1_grp[:].rearrange("p t m j -> p (t m j)")
         )
 
+        for j in range(PACK - 1):
+            gather(j, 0, S)
+
         gather(PACK - 1, 0, half)
         x_quant(0)
         x_quant(1)
@@ -93,13 +91,11 @@ def tile_picked_sub_mlp_gelu_sub_e_kernel(tc, xT, w1, w2, gate, offs, pos1, pos2
         x_quant(2)
         x_quant(3)
 
-        ident = keep.tile([P, P], BF16, name="ident")
+        ident = keep.tile([P, P], F32, name="ident")
         make_identity(nc, ident[:])
-        warm_ps = psum.tile([P, P], BF16, name="warm_ps", tag="y_tail1")
-        w1_flat = w1_grp[:].rearrange("p t m j -> p (t m j)")
-        for i in range(20):
-            c0 = i % 16 * P
-            nc.tensor.transpose(warm_ps[:], w1_flat[:, c0 : c0 + P], ident[:])
+        warm_ps = psum.tile([P, P], F32, name="warm_ps", tag="y_tail1")
+        for t0 in range(0, T, P):
+            nc.tensor.transpose(warm_ps[:], x_raw[2][:, t0 : t0 + P], ident[:])
 
         w2_codes = keep.tile([P, N], U32, name="w2_codes", align_bytes=64)
         w2_scales = keep.tile([P, N], U8, name="w2_scales", align_bytes=64)
@@ -199,6 +195,6 @@ def tile_picked_sub_mlp_gelu_sub_e_kernel(tc, xT, w1, w2, gate, offs, pos1, pos2
         finish(0, 2)
         term(2, 1)
         term(3, 0)
-        finish(2, 3)
         term(3, 1)
+        finish(2, 3)
         finish(3, 4)

from contextlib import ExitStack

import concourse.mybir as mybir
from concourse.masks import make_identity

K, T, D, S, V, H, N = 512, 2048, 2, 512, 256, 512, 512
FLOPS = 2 * S * (K * H + H * N) + 3 * N * V

F32 = mybir.dt.float32
BF16 = mybir.dt.bfloat16
U32 = mybir.dt.uint32
U16 = mybir.dt.uint16
U8 = mybir.dt.uint8
FP8X4 = mybir.dt.float8_e4m3fn_x4
ACT = mybir.ActivationFunctionType
ALU = mybir.AluOpType

P = 128
PACK = 4
BLOCKS = N // P


def tile_picked_sub_mlp_gelu_sub_e_kernel(tc, xT, w1, w2, gate, offs, pos1, pos2, out):
    nc = tc.nc
    with ExitStack() as ctx:
        lists = ctx.enter_context(tc.tile_pool(name="lists", bufs=1))
        keep = ctx.enter_context(tc.tile_pool(name="keep", bufs=1))
        psum = ctx.enter_context(tc.psum_pool(name="psum", bufs=1))

        offs_sb = lists.tile([P, S // 16], U16, name="offs_sb")
        pos_sb = [lists.tile([P, V // 16], U16, name=f"pos_sb{d}") for d in range(D)]

        warm = keep.tile([P, 1], F32, name="warm")
        nc.vector.memset(warm[:], 0.0)
        warm_out = keep.tile([P, 1], F32, name="warm_out")
        nc.scalar.activation(warm_out[:], warm[:], ACT.Gelu_apprx_tanh)

        x_rows = xT.rearrange("(p j) t -> p j t", j=PACK)
        w1_rows = w1.rearrange("(p j) c -> p j c", j=PACK)
        w2_rows = w2.rearrange("(p j) c -> p j c", j=PACK)
        x_raw = [keep.tile([P, T], F32, name=f"x_raw{j}") for j in range(PACK)]
        w1_raw = keep.tile([P, PACK, H], F32, name="w1_raw")
        w2_raw = [keep.tile([P, PACK, N // 2], F32, name=f"w2_raw{u}") for u in range(2)]
        gate_sb = [keep.tile([P, D, V], F32, name=f"gate_sb{b}") for b in range(BLOCKS)]
        nc.sync.dma_start(w1_raw[:], w1_rows)
        nc.sync.dma_start(offs_sb[:], offs)
        for j in range(PACK):
            nc.sync.dma_start(x_raw[j][:], x_rows[:, j, :])
        for u in range(2):
            nc.sync.dma_start(w2_raw[u][:], w2_rows[:, :, u * N // 2 : (u + 1) * N // 2])
        nc.sync.dma_start(pos_sb[0][:], pos1)
        nc.sync.dma_start(pos_sb[1][:], pos2)
        for b in range(BLOCKS):
            nc.sync.dma_start(gate_sb[b][:], gate[:, b * P : (b + 1) * P, :].rearrange("d p v -> p d v"))

        half = S // 2
        x_grp = keep.tile([P, S, PACK], BF16, name="x_grp", align_bytes=64)
        x_codes = keep.tile([P, S], U32, name="x_codes", align_bytes=64)
        x_scales = keep.tile([P, S], U8, name="x_scales", align_bytes=64)

        def gather(j, s0, s1):
            nc.vector.tensor_copy(x_grp[:, s0:s1, j], x_raw[j][:].indirect(offs_sb[:, s0 // 16 : s1 // 16]))

        def x_quant(q):
            toks = slice(q * P, (q + 1) * P)
            nc.vector.quantize_mx(
                out=x_codes[:, toks].bitcast(FP8X4),
                scales=x_scales[:, toks],
                in_=x_grp[:, toks, :].rearrange("p s j -> p (s j)"),
            )

        w1_grp = keep.tile([P, PACK, P, PACK], BF16, name="w1_grp", align_bytes=64)
        for copy, m0 in ((nc.scalar.copy, 0), (nc.vector.tensor_copy, P // 2)):
            copy(
                w1_grp[:, :, m0 : m0 + P // 2, :].rearrange("p t m j -> p m t j"),
                w1_raw[:, :, PACK * m0 : PACK * (m0 + P // 2)].rearrange("p j (m t) -> p m t j", t=PACK),
            )
        w1_codes = keep.tile([P, H], U32, name="w1_codes", align_bytes=64)
        w1_scales = keep.tile([P, H], U8, name="w1_scales", align_bytes=64)
        nc.vector.quantize_mx(
            out=w1_codes[:].bitcast(FP8X4), scales=w1_scales[:], in_=w1_grp[:].rearrange("p t m j -> p (t m j)")
        )

        for j in range(PACK - 1):
            gather(j, 0, S)

        gather(PACK - 1, 0, half)
        x_quant(0)
        x_quant(1)
        gather(PACK - 1, half - 32, S)
        x_quant(2)
        x_quant(3)

        ident = keep.tile([P, P], F32, name="ident")
        make_identity(nc, ident[:])
        warm_ps = psum.tile([P, P], F32, name="warm_ps", tag="y_tail1")
        for t0 in range(0, T, P):
            nc.tensor.transpose(warm_ps[:], x_raw[2][:, t0 : t0 + P], ident[:])

        w2_codes = keep.tile([P, N], U32, name="w2_codes", align_bytes=64)
        w2_scales = keep.tile([P, N], U8, name="w2_scales", align_bytes=64)

        def w2_block(copy, b, tag):
            c0 = b * P
            r0 = c0 % (N // 2)
            w2_grp = keep.tile([P, P, PACK], BF16, name=f"w2_grp{b}", tag=tag, align_bytes=64)
            copy(w2_grp[:], w2_raw[b // 2][:, :, r0 : r0 + P].rearrange("p j c -> p c j"))
            nc.vector.quantize_mx(
                out=w2_codes[:, c0 : c0 + P].bitcast(FP8X4),
                scales=w2_scales[:, c0 : c0 + P],
                in_=w2_grp[:].rearrange("p c j -> p (c j)"),
            )

        h_codes = keep.tile([P, S], U32, name="h_codes", align_bytes=64)
        h_scales = keep.tile([P, S], U8, name="h_scales", align_bytes=64)

        def layer1(q):
            toks = slice(q * P, (q + 1) * P)
            acc = psum.tile([P, PACK, P], F32, name=f"acc1_{q}")
            for t in range(PACK):
                cols = slice(t * P, (t + 1) * P)
                nc.tensor.matmul_mx(
                    out=acc[:, t, :],
                    lhsT=w1_codes[:, cols].bitcast(FP8X4),
                    lhsT_scale=w1_scales[:, cols],
                    rhs=x_codes[:, toks].bitcast(FP8X4),
                    rhs_scale=x_scales[:, toks],
                    start=True,
                    stop=True,
                )
            h_grp = keep.tile([P, P, PACK], BF16, name=f"h_grp{q}", tag=f"h_grp{q}", align_bytes=64)
            nc.scalar.activation(h_grp[:], acc[:].rearrange("p t n -> p n t"), ACT.Gelu_apprx_tanh)
            nc.vector.quantize_mx(
                out=h_codes[:, toks].bitcast(FP8X4),
                scales=h_scales[:, toks],
                in_=h_grp[:].rearrange("p n t -> p (n t)"),
            )

        y_sb = [keep.tile([P, S], F32, name=f"y_sb{b}") for b in range(BLOCKS)]

        def layer2(acc, b, t0, t1):
            cols = slice(b * P, (b + 1) * P)
            nc.tensor.matmul_mx(
                out=acc,
                lhsT=w2_codes[:, cols].bitcast(FP8X4),
                lhsT_scale=w2_scales[:, cols],
                rhs=h_codes[:, t0:t1].bitcast(FP8X4),
                rhs_scale=h_scales[:, t0:t1],
                start=True,
                stop=True,
            )

        head = S - P
        y_head = [psum.tile([P, head], F32, name=f"y_head{b}") for b in range(2)]
        y_tail = [psum.tile([P, P], F32, name=f"y_tail{b}", tag=f"y_tail{b}") for b in range(2)]
        w2_block(nc.scalar.copy, 0, "w2_grp0")
        layer1(0)
        layer1(1)
        w2_block(nc.vector.tensor_copy, 1, "w2_grp1")
        w2_block(nc.vector.tensor_copy, 2, "w2_grp2")
        layer1(2)
        layer1(3)
        w2_block(nc.vector.tensor_copy, 3, "w2_grp3")
        for b in range(2):
            layer2(y_head[b][:, 0:half], b, 0, half)
            layer2(y_head[b][:, half:head], b, half, head)
        nc.vector.tensor_copy(y_sb[0][:, 0:head], y_head[0][:])
        for b in range(2):
            layer2(y_tail[b][:], b, head, S)
        nc.scalar.copy(y_sb[0][:, head:S], y_tail[0][:])
        nc.scalar.copy(y_sb[1][:, 0:head], y_head[1][:])
        nc.scalar.copy(y_sb[1][:, head:S], y_tail[1][:])
        for b in range(2, BLOCKS):
            y_acc = psum.tile([P, S], F32, name=f"y_acc{b}", tag=f"acc1_{b - 2}")
            layer2(y_acc[:], b, 0, S)
            nc.scalar.copy(y_sb[b][:], y_acc[:])

        terms = [keep.tile([P, BLOCKS, V], F32, name=f"terms{d}") for d in range(D)]
        total = keep.tile([P, BLOCKS, V], F32, name="total")
        out_rows = out.rearrange("(b p) v -> p b v", p=P)

        def term(b, d):
            nc.vector.tensor_tensor(
                terms[d][:, b, :], y_sb[b][:].indirect(pos_sb[d][:]), gate_sb[b][:, d, :], ALU.mult
            )

        def finish(b0, b1):
            nc.vector.tensor_tensor(total[:, b0:b1, :], terms[0][:, b0:b1, :], terms[1][:, b0:b1, :], ALU.add)
            nc.sync.dma_start(out_rows[:, b0:b1, :], total[:, b0:b1, :])

        for b in (0, 1):
            for d in range(D):
                term(b, d)
        term(2, 0)
        finish(0, 2)
        term(2, 1)
        term(3, 0)
        term(3, 1)
        finish(2, 3)
        finish(3, 4)
